import numpy as np
import ml_dtypes


def mxq(x, axis, fmt="e4m3"):
    dtype, down = {"e4m3": (ml_dtypes.float8_e4m3fn, 7), "e5m2": (ml_dtypes.float8_e5m2, 14)}[fmt]
    v = np.moveaxis(np.asarray(x, np.float32).astype(ml_dtypes.bfloat16).astype(np.float64), axis, -1)
    blocks = v.reshape(v.shape[:-1] + (-1, 32))
    amax = np.abs(blocks).max(-1, keepdims=True)
    byte = np.maximum(np.where(amax > 0, np.frexp(amax)[1] - 1 + 127, 0) - down, 1)
    scale = np.exp2(byte - 127.0)
    codes = (blocks / scale).astype(np.float32).astype(dtype).astype(np.float64)
    return np.moveaxis((codes * scale).reshape(v.shape), -1, axis)


WIDE = False


def mx_kscale(k):
    if not WIDE:
        return np.ones(k)
    levels = np.array([18, -18])
    if k % 512:
        return np.exp2(np.random.permutation(np.resize(levels, k // 32))).repeat(32)
    a = np.empty((k // 512, 16))
    for p in range(k // 512):
        a[p, :8] = np.random.permutation(np.resize(levels, 8))
        for g in range(8):
            far = levels[np.abs(levels - a[p, g]) >= 10]
            a[p, g + 8] = far[np.random.randint(len(far))]
    return np.exp2(a.ravel()).repeat(32)


def f64(x):
    return np.asarray(x).astype(np.float64)


def striped(idx):
    return np.tile(np.asarray(idx).reshape(-1, 16).T, (8, 1)).astype(np.uint16)


def unstriped(offs):
    return offs[:16].T.reshape(-1).astype(np.int64)


T, C, D, DV = 1024, 512, 512, 512
BETA = 0.25


def setup_inputs():
    n = np.random.standard_normal
    grid = lambda v: np.clip(np.round(v * 16) / 16, -4, 4)
    v = mx_kscale(DV)[:, None]
    return {
        "zT": (grid(n((DV, T))) * v).astype(np.float32),
        "cb": (grid(n((DV, C))) * v).astype(np.float32),
        "wm": (n((DV, D)) / np.sqrt(DV) / v).astype(np.float32),
        "offs": striped(np.random.randint(0, C, T)),
    }


def reference(zT, cb, wm, offs):
    e = f64(zT) - f64(cb)[:, unstriped(offs)]
    g = BETA * e
    return mxq(f64(wm), 0, "e4m3").T @ mxq(g, 0, "e5m2")

@@ -1,0 +1,139 @@
+from contextlib import ExitStack
+
+import concourse.mybir as mybir
+
+T, C, D, DV = 1024, 512, 512, 512
+BETA = 0.25
+FLOPS = 2 * DV * D * T
+
+F32 = mybir.dt.float32
+BF16 = mybir.dt.bfloat16
+U32 = mybir.dt.uint32
+U16 = mybir.dt.uint16
+U8 = mybir.dt.uint8
+E4M3 = mybir.dt.float8_e4m3fn_x4
+E5M2 = mybir.dt.float8_e5m2_x4
+SUB = mybir.AluOpType.subtract
+MULT = mybir.AluOpType.mult
+COPY = mybir.ActivationFunctionType.Copy
+
+P = 128
+PACK = 4
+HALF = 512
+CH = 256
+RUN = 4
+
+
+def tile_attend_gvq_c_x_kernel(tc, zT, cb, wm, offs, out):
+    nc = tc.nc
+    with ExitStack() as ctx:
+        lists = ctx.enter_context(tc.tile_pool(name="lists", bufs=1))
+        keep = ctx.enter_context(tc.tile_pool(name="keep", bufs=1))
+        psum = ctx.enter_context(tc.psum_pool(name="psum", bufs=1))
+
+        codes = lists.tile([P, T // 16], U16, name="codes")
+        nc.sync.dma_start(codes[:], offs)
+
+        cb_rows = cb.rearrange("(p j) c -> p j c", j=PACK)
+        z_rows = zT.rearrange("(p j) t -> p j t", j=PACK)
+        w_rows = wm.rearrange("(p j) d -> p j d", j=PACK)
+
+        def planes(tile):
+            return tile[:].rearrange("p (j c) -> p j c", j=PACK)
+
+        book = [keep.tile([P, C], F32, name=f"book{j}") for j in range(PACK)]
+        z_first = [keep.tile([P, HALF], F32, name=f"z_first{j}") for j in range(PACK)]
+        z_late = [keep.tile([P, PACK * CH], F32, name=f"z_late{q}") for q in range(2)]
+        w_raw = [keep.tile([P, PACK * CH], F32, name=f"w_raw{s}", align_bytes=64) for s in range(2)]
+        for j in range(PACK):
+            nc.sync.dma_start(book[j][:], cb_rows[:, j, :])
+            nc.sync.dma_start(z_first[j][:], z_rows[:, j, 0:HALF])
+        nc.sync.dma_start(planes(z_late[0]), z_rows[:, :, HALF : HALF + CH])
+        nc.sync.dma_start(planes(w_raw[0]), w_rows[:, :, 0:CH])
+        nc.sync.dma_start(planes(w_raw[1]), w_rows[:, :, CH:D])
+        nc.sync.dma_start(planes(z_late[1]), z_rows[:, :, HALF + CH : T])
+
+        diff = [keep.tile([P, PACK * CH], F32, name=f"diff{q}", align_bytes=64) for q in range(3)]
+        diff.append(diff[1])
+        g_words = [keep.tile([P, HALF], U32, name=f"g_words{h}", align_bytes=64) for h in range(2)]
+        g_scales = [keep.tile([P, HALF], U8, name=f"g_scales{h}", align_bytes=64) for h in range(2)]
+        w_words = keep.tile([P, D], U32, name="w_words", align_bytes=64)
+        w_scales = keep.tile([P, D], U8, name="w_scales", align_bytes=64)
+        g_bf = [keep.tile([P, PACK * CH], BF16, name=f"g_bf{q}", align_bytes=64)[:] for q in range(2)]
+        g_bf.append(w_raw[1][:, 0 : PACK * CH // 2].bitcast(BF16))
+        g_last = [keep.tile([P, PACK * CH // 2], BF16, name=f"g_last{s}", align_bytes=64)[:] for s in range(2)]
+        w_bf = [diff[1][:, s * 512 : (s + 1) * 512].bitcast(BF16) for s in range(2)]
+
+        def look_up(q, j, z, a=0, b=CH):
+            cols = slice((q * CH + a) // 16, (q * CH + b) // 16)
+            nc.vector.tensor_tensor(
+                diff[q][:, j * CH + a : j * CH + b], book[j][:].indirect(codes[:, cols]), z, SUB
+            )
+
+        def woven(dst):
+            return dst.rearrange("p (c i j) -> p c j i", i=RUN, j=PACK)
+
+        def runs(src):
+            return src.rearrange("p j (c i) -> p c j i", i=RUN)
+
+        def weave_g(dst, src, on_vector):
+            if on_vector:
+                nc.vector.tensor_scalar(woven(dst), runs(src), -BETA, None, MULT)
+            else:
+                nc.scalar.activation(woven(dst), runs(src), COPY, scale=-BETA)
+
+        def quant_g(lo, width, src):
+            h, lo = divmod(lo, HALF)
+            cols = slice(lo, lo + width)
+            nc.vector.quantize_mx(g_words[h][:, cols].bitcast(E5M2), g_scales[h][:, cols], src)
+
+        def quant_w(s):
+            cols = slice(s * CH, (s + 1) * CH)
+            nc.vector.quantize_mx(w_words[:, cols].bitcast(E4M3), w_scales[:, cols], w_bf[s])
+
+        def product(h, engines):
+            for m in range(D // P):
+                rows = slice(m * P, (m + 1) * P)
+                bank = psum.tile([P, HALF], F32, name=f"bank{h}_{m}")
+                nc.tensor.matmul_mx(
+                    bank[:],
+                    lhsT=w_words[:, rows].bitcast(E4M3),
+                    lhsT_scale=w_scales[:, rows],
+                    rhs=g_words[h][:].bitcast(E5M2),
+                    rhs_scale=g_scales[h][:],
+                    start=True,
+                    stop=True,
+                )
+                res = keep.tile([P, HALF], F32, name=f"res{h}_{m}")
+                if engines[m] == "v":
+                    nc.vector.tensor_copy(res[:], bank[:])
+                else:
+                    nc.scalar.copy(res[:], bank[:])
+                nc.sync.dma_start(out[rows, h * HALF : (h + 1) * HALF], res[:])
+
+        for j in range(PACK):
+            for q in range(2):
+                look_up(q, j, z_first[j][:, q * CH : (q + 1) * CH])
+        weave_g(g_bf[0], planes(diff[0]), False)
+        weave_g(g_bf[1], planes(diff[1]), False)
+        for j in range(PACK):
+            look_up(2, j, z_late[0][:, j * CH : (j + 1) * CH])
+        quant_g(0, CH, g_bf[0])
+        quant_g(CH, CH, g_bf[1])
+        for s in range(2):
+            nc.scalar.copy(woven(w_bf[s]), runs(planes(w_raw[s])))
+        weave_g(g_bf[2], planes(diff[2]), False)
+        quant_w(0)
+        look_up(3, 0, z_late[1][:, 0:CH])
+        look_up(3, 1, z_late[1][:, CH : 2 * CH])
+        quant_w(1)
+        look_up(3, 2, z_late[1][:, 2 * CH : 3 * CH])
+        quant_g(2 * CH, CH, g_bf[2])
+        look_up(3, 3, z_late[1][:, 3 * CH : 3 * CH + 128], 0, 128)
+        look_up(3, 3, z_late[1][:, 3 * CH + 128 : 4 * CH], 128, 256)
+        weave_g(g_last[0], planes(diff[3])[:, :, 0:128], False)
+        weave_g(g_last[1], planes(diff[3])[:, :, 128:256], True)
+        product(0, "ssss")
+        quant_g(3 * CH, 128, g_last[0])
+        quant_g(3 * CH + 128, 128, g_last[1])
+        product(1, "vsvs")

@@ -38,37 +38,48 @@ def tile_attend_gvq_c_x_kernel(tc, zT, cb, wm, offs, out):
         z_rows = zT.rearrange("(p j) t -> p j t", j=PACK)
         w_rows = wm.rearrange("(p j) d -> p j d", j=PACK)
 
-        def planes(tile):
-            return tile[:].rearrange("p (j c) -> p j c", j=PACK)
+        def planes(ap):
+            return ap.rearrange("p (j c) -> p j c", j=PACK)
 
-        book = [keep.tile([P, C], F32, name=f"book{j}") for j in range(PACK)]
+        STEP = 768
+        shared = keep.tile([P, PACK * STEP], F32, name="shared", align_bytes=64)
+        diff_late = planes(shared[:])[:, :, 0:HALF]
+        diff_first = planes(keep.tile([P, PACK * HALF], F32, name="diff_first")[:])
+        w_bf = [shared[:, lo : lo + HALF].bitcast(BF16) for lo in (STEP + 384, 2 * STEP + CH)]
+
+        book = [keep.tile([P, 2 * C], F32, name=f"book{j}") for j in range(PACK)]
+        z_head = keep.tile([P, CH], F32, name="z_head")
         z_first = [keep.tile([P, HALF], F32, name=f"z_first{j}") for j in range(PACK)]
-        z_late = [keep.tile([P, PACK * CH], F32, name=f"z_late{q}") for q in range(2)]
-        w_raw = [keep.tile([P, PACK * CH], F32, name=f"w_raw{s}", align_bytes=64) for s in range(2)]
+        z_late = [keep.tile([P, HALF], F32, name=f"z_late{j}")[:] for j in (0, 1, 3)]
+        z_late.insert(2, diff_late[:, 3, :])
+        w_raw = keep.tile([P, PACK, D], F32, name="w_raw")
         for j in range(PACK):
-            nc.sync.dma_start(book[j][:], cb_rows[:, j, :])
-            nc.sync.dma_start(z_first[j][:], z_rows[:, j, 0:HALF])
-        nc.sync.dma_start(planes(z_late[0]), z_rows[:, :, HALF : HALF + CH])
-        nc.sync.dma_start(planes(w_raw[0]), w_rows[:, :, 0:CH])
-        nc.sync.dma_start(planes(w_raw[1]), w_rows[:, :, CH:D])
-        nc.sync.dma_start(planes(z_late[1]), z_rows[:, :, HALF + CH : T])
+            nc.gpsimd.memset(book[j][:, C : 2 * C], 0.0)
+            nc.sync.dma_start(book[j][:, 0:C], cb_rows[:, j, :])
+            if j == 0:
+                nc.sync.dma_start(z_head[:], z_rows[:, 0, 0:CH])
+                nc.sync.dma_start(z_first[0][:, CH:HALF], z_rows[:, 0, CH:HALF])
+            else:
+                nc.sync.dma_start(z_first[j][:], z_rows[:, j, 0:HALF])
+        for j in range(PACK):
+            if j == 1:
+                nc.sync.dma_start(w_raw[:], w_rows)
+            nc.sync.dma_start(z_late[j], z_rows[:, j, HALF:T])
 
-        diff = [keep.tile([P, PACK * CH], F32, name=f"diff{q}", align_bytes=64) for q in range(3)]
-        diff.append(diff[1])
-        g_words = [keep.tile([P, HALF], U32, name=f"g_words{h}", align_bytes=64) for h in range(2)]
-        g_scales = [keep.tile([P, HALF], U8, name=f"g_scales{h}", align_bytes=64) for h in range(2)]
+        g_words = keep.tile([P, T], U32, name="g_words", align_bytes=64)
+        g_scales = keep.tile([P, T], U8, name="g_scales", align_bytes=64)
         w_words = keep.tile([P, D], U32, name="w_words", align_bytes=64)
         w_scales = keep.tile([P, D], U8, name="w_scales", align_bytes=64)
-        g_bf = [keep.tile([P, PACK * CH], BF16, name=f"g_bf{q}", align_bytes=64)[:] for q in range(2)]
-        g_bf.append(w_raw[1][:, 0 : PACK * CH // 2].bitcast(BF16))
-        g_last = [keep.tile([P, PACK * CH // 2], BF16, name=f"g_last{s}", align_bytes=64)[:] for s in range(2)]
-        w_bf = [diff[1][:, s * 512 : (s + 1) * 512].bitcast(BF16) for s in range(2)]
+        g_bf = [keep.tile([P, PACK * CH], BF16, name=f"g_bf{q}", align_bytes=64)[:] for q in range(3)]
+        g_last = [keep.tile([P, PACK * 128], BF16, name="g_last0", align_bytes=64)[:], g_bf[2][:, 0 : PACK * 128]]
 
-        def look_up(q, j, z, a=0, b=CH):
-            cols = slice((q * CH + a) // 16, (q * CH + b) // 16)
-            nc.vector.tensor_tensor(
-                diff[q][:, j * CH + a : j * CH + b], book[j][:].indirect(codes[:, cols]), z, SUB
-            )
+        def look_up(j, lo, hi, z=None):
+            half, a = divmod(lo, HALF)
+            b = a + hi - lo
+            dst = (diff_first, diff_late)[half][:, j, a:b]
+            if z is None:
+                z = (z_first, z_late)[half][j][:, a:b]
+            nc.vector.tensor_tensor(dst, book[j][:].indirect(codes[:, lo // 16 : hi // 16]), z, SUB)
 
         def woven(dst):
             return dst.rearrange("p (c i j) -> p c j i", i=RUN, j=PACK)
@@ -83,57 +94,70 @@ def tile_attend_gvq_c_x_kernel(tc, zT, cb, wm, offs, out):
                 nc.scalar.activation(woven(dst), runs(src), COPY, scale=-BETA)
 
         def quant_g(lo, width, src):
-            h, lo = divmod(lo, HALF)
             cols = slice(lo, lo + width)
-            nc.vector.quantize_mx(g_words[h][:, cols].bitcast(E5M2), g_scales[h][:, cols], src)
+            nc.vector.quantize_mx(g_words[:, cols].bitcast(E5M2), g_scales[:, cols], src)
 
         def quant_w(s):
             cols = slice(s * CH, (s + 1) * CH)
             nc.vector.quantize_mx(w_words[:, cols].bitcast(E4M3), w_scales[:, cols], w_bf[s])
 
-        def product(h, engines):
-            for m in range(D // P):
-                rows = slice(m * P, (m + 1) * P)
-                bank = psum.tile([P, HALF], F32, name=f"bank{h}_{m}")
-                nc.tensor.matmul_mx(
-                    bank[:],
-                    lhsT=w_words[:, rows].bitcast(E4M3),
-                    lhsT_scale=w_scales[:, rows],
-                    rhs=g_words[h][:].bitcast(E5M2),
-                    rhs_scale=g_scales[h][:],
-                    start=True,
-                    stop=True,
-                )
-                res = keep.tile([P, HALF], F32, name=f"res{h}_{m}")
-                if engines[m] == "v":
-                    nc.vector.tensor_copy(res[:], bank[:])
-                else:
-                    nc.scalar.copy(res[:], bank[:])
-                nc.sync.dma_start(out[rows, h * HALF : (h + 1) * HALF], res[:])
+        def product(m, lo, new, bank_tag, on_vector, res=None):
+            rows = slice(m * P, (m + 1) * P)
+            cols = slice(lo, lo + HALF)
+            bank = psum.tile([P, HALF], F32, name=f"bank{m}_{lo}", tag=bank_tag)
+            nc.tensor.matmul_mx(
+                bank[:],
+                lhsT=w_words[:, rows].bitcast(E4M3),
+                lhsT_scale=w_scales[:, rows],
+                rhs=g_words[:, cols].bitcast(E5M2),
+                rhs_scale=g_scales[:, cols],
+                start=True,
+                stop=True,
+            )
+            if res is None:
+                res = keep.tile([P, new], F32, name=f"res{m}_{lo}")[:]
+            if on_vector:
+                nc.vector.tensor_copy(res, bank[:, HALF - new : HALF])
+            else:
+                nc.scalar.copy(res, bank[:, HALF - new : HALF])
+            nc.sync.dma_start(out[rows, lo + HALF - new : lo + HALF], res)
+            return res
 
-        for j in range(PACK):
-            for q in range(2):
-                look_up(q, j, z_first[j][:, q * CH : (q + 1) * CH])
-        weave_g(g_bf[0], planes(diff[0]), False)
-        weave_g(g_bf[1], planes(diff[1]), False)
-        for j in range(PACK):
-            look_up(2, j, z_late[0][:, j * CH : (j + 1) * CH])
+        look_up(0, 0, CH, z_head[:])
+        look_up(0, CH, HALF)
+        look_up(1, 0, HALF)
+        look_up(2, 0, HALF)
+        look_up(3, 0, CH)
+        look_up(3, CH, HALF)
+        weave_g(g_bf[0], diff_first[:, :, 0:CH], False)
+        weave_g(g_bf[1], diff_first[:, :, CH:HALF], False)
+        look_up(0, HALF, T)
         quant_g(0, CH, g_bf[0])
         quant_g(CH, CH, g_bf[1])
+        look_up(1, 2 * CH, 3 * CH)
         for s in range(2):
-            nc.scalar.copy(woven(w_bf[s]), runs(planes(w_raw[s])))
-        weave_g(g_bf[2], planes(diff[2]), False)
+            nc.scalar.copy(woven(w_bf[s]), runs(w_raw[:, :, s * CH : (s + 1) * CH]))
         quant_w(0)
-        look_up(3, 0, z_late[1][:, 0:CH])
-        look_up(3, 1, z_late[1][:, CH : 2 * CH])
+        look_up(1, 3 * CH, T)
+        look_up(2, 2 * CH, 3 * CH)
+        look_up(3, 2 * CH, 3 * CH)
         quant_w(1)
-        look_up(3, 2, z_late[1][:, 2 * CH : 3 * CH])
+        look_up(2, 3 * CH, T)
+        look_up(3, 3 * CH, 3 * CH + 128)
+        look_up(3, 3 * CH + 128, T)
+        product(0, 0, HALF, "b0", False)
+        product(1, 0, HALF, "b1", False)
+        weave_g(g_bf[2], diff_late[:, :, 0:CH], False)
+        product(2, 0, HALF, "b2", False)
+        weave_g(g_last[0], diff_late[:, :, CH : CH + 128], False)
         quant_g(2 * CH, CH, g_bf[2])
-        look_up(3, 3, z_late[1][:, 3 * CH : 3 * CH + 128], 0, 128)
-        look_up(3, 3, z_late[1][:, 3 * CH + 128 : 4 * CH], 128, 256)
-        weave_g(g_last[0], planes(diff[3])[:, :, 0:128], False)
-        weave_g(g_last[1], planes(diff[3])[:, :, 128:256], True)
-        product(0, "ssss")
+        weave_g(g_last[1], diff_late[:, :, CH + 128 : HALF], True)
         quant_g(3 * CH, 128, g_last[0])
         quant_g(3 * CH + 128, 128, g_last[1])
-        product(1, "vsvs")
+        product(3, 0, HALF, "b3", False)
+        product(0, CH, CH, "b4", True, g_last[1].bitcast(F32))
+        product(1, CH, CH, "b5", True, g_last[0].bitcast(F32))
+        product(2, HALF, HALF, "b6", True)
+        product(3, HALF, HALF, "b7", False)
+        product(0, HALF, CH, "b0", True)
+        product(1, HALF, CH, "b1", False)

@@ -19,9 +19,12 @@ COPY = mybir.ActivationFunctionType.Copy
 
 P = 128
 PACK = 4
+BAND = 16
 HALF = 512
-CH = 256
+CHUNK = 256
+PIECE = 128
 RUN = 4
+STEP = HALF + CHUNK
 
 
 def tile_attend_gvq_c_x_kernel(tc, zT, cb, wm, offs, out):
@@ -31,7 +34,7 @@ def tile_attend_gvq_c_x_kernel(tc, zT, cb, wm, offs, out):
         keep = ctx.enter_context(tc.tile_pool(name="keep", bufs=1))
         psum = ctx.enter_context(tc.psum_pool(name="psum", bufs=1))
 
-        codes = lists.tile([P, T // 16], U16, name="codes")
+        codes = lists.tile([P, T // BAND], U16, name="codes")
         nc.sync.dma_start(codes[:], offs)
 
         cb_rows = cb.rearrange("(p j) c -> p j c", j=PACK)
@@ -41,45 +44,45 @@ def tile_attend_gvq_c_x_kernel(tc, zT, cb, wm, offs, out):
         def planes(ap):
             return ap.rearrange("p (j c) -> p j c", j=PACK)
 
-        STEP = 768
         shared = keep.tile([P, PACK * STEP], F32, name="shared", align_bytes=64)
         diff_late = planes(shared[:])[:, :, 0:HALF]
-        diff_first = planes(keep.tile([P, PACK * HALF], F32, name="diff_first")[:])
-        w_bf = [shared[:, lo : lo + HALF].bitcast(BF16) for lo in (STEP + 384, 2 * STEP + CH)]
+        diff_early = planes(keep.tile([P, PACK * HALF], F32, name="diff_early")[:])
+        w_bf = [
+            shared[:, lo : lo + PACK * CHUNK // 2].bitcast(BF16) for lo in (2 * STEP - CHUNK, 2 * STEP + CHUNK)
+        ]
 
         book = [keep.tile([P, 2 * C], F32, name=f"book{j}") for j in range(PACK)]
-        z_head = keep.tile([P, CH], F32, name="z_head")
-        z_first = [keep.tile([P, HALF], F32, name=f"z_first{j}") for j in range(PACK)]
+        z_head = [keep.tile([P, CHUNK], F32, name=f"z_head{q}") for q in range(2)]
+        z_early = {j: keep.tile([P, HALF], F32, name=f"z_early{j}") for j in range(1, PACK)}
         z_late = [keep.tile([P, HALF], F32, name=f"z_late{j}")[:] for j in (0, 1, 3)]
         z_late.insert(2, diff_late[:, 3, :])
-        w_raw = keep.tile([P, PACK, D], F32, name="w_raw")
+        w_raw = [keep.tile([P, PACK, CHUNK], F32, name=f"w_raw{s}") for s in range(2)]
+
         for j in range(PACK):
             nc.gpsimd.memset(book[j][:, C : 2 * C], 0.0)
             nc.sync.dma_start(book[j][:, 0:C], cb_rows[:, j, :])
             if j == 0:
-                nc.sync.dma_start(z_head[:], z_rows[:, 0, 0:CH])
-                nc.sync.dma_start(z_first[0][:, CH:HALF], z_rows[:, 0, CH:HALF])
+                for q in range(2):
+                    nc.sync.dma_start(z_head[q][:], z_rows[:, 0, q * CHUNK : (q + 1) * CHUNK])
             else:
-                nc.sync.dma_start(z_first[j][:], z_rows[:, j, 0:HALF])
-        for j in range(PACK):
-            if j == 1:
-                nc.sync.dma_start(w_raw[:], w_rows)
-            nc.sync.dma_start(z_late[j], z_rows[:, j, HALF:T])
+                nc.sync.dma_start(z_early[j][:], z_rows[:, j, 0:HALF])
+        nc.sync.dma_start(z_late[0], z_rows[:, 0, HALF:T])
+        nc.sync.dma_start(z_late[1], z_rows[:, 1, HALF:T])
+        for s in range(2):
+            nc.sync.dma_start(w_raw[s][:], w_rows[:, :, s * CHUNK : (s + 1) * CHUNK])
+            nc.sync.dma_start(z_late[2 + s], z_rows[:, 2 + s, HALF:T])
 
         g_words = keep.tile([P, T], U32, name="g_words", align_bytes=64)
         g_scales = keep.tile([P, T], U8, name="g_scales", align_bytes=64)
         w_words = keep.tile([P, D], U32, name="w_words", align_bytes=64)
         w_scales = keep.tile([P, D], U8, name="w_scales", align_bytes=64)
-        g_bf = [keep.tile([P, PACK * CH], BF16, name=f"g_bf{q}", align_bytes=64)[:] for q in range(3)]
-        g_last = [keep.tile([P, PACK * 128], BF16, name="g_last0", align_bytes=64)[:], g_bf[2][:, 0 : PACK * 128]]
+        g_early = keep.tile([P, PACK * HALF], BF16, name="g_early", align_bytes=64)
+        g_late = keep.tile([P, PACK * CHUNK], BF16, name="g_late", align_bytes=64)
 
-        def look_up(j, lo, hi, z=None):
-            half, a = divmod(lo, HALF)
-            b = a + hi - lo
-            dst = (diff_first, diff_late)[half][:, j, a:b]
-            if z is None:
-                z = (z_first, z_late)[half][j][:, a:b]
-            nc.vector.tensor_tensor(dst, book[j][:].indirect(codes[:, lo // 16 : hi // 16]), z, SUB)
+        def look_up(j, lo, hi, z):
+            half, first = divmod(lo, HALF)
+            dst = (diff_early, diff_late)[half][:, j, first : first + hi - lo]
+            nc.vector.tensor_tensor(dst, book[j][:].indirect(codes[:, lo // BAND : hi // BAND]), z, SUB)
 
         def woven(dst):
             return dst.rearrange("p (c i j) -> p c j i", i=RUN, j=PACK)
@@ -87,21 +90,20 @@ def tile_attend_gvq_c_x_kernel(tc, zT, cb, wm, offs, out):
         def runs(src):
             return src.rearrange("p j (c i) -> p c j i", i=RUN)
 
-        def weave_g(dst, src, on_vector):
-            if on_vector:
-                nc.vector.tensor_scalar(woven(dst), runs(src), -BETA, None, MULT)
-            else:
-                nc.scalar.activation(woven(dst), runs(src), COPY, scale=-BETA)
+        def weave_g_on_scalar(dst, src):
+            nc.scalar.activation(woven(dst), runs(src), COPY, scale=-BETA)
 
-        def quant_g(lo, width, src):
-            cols = slice(lo, lo + width)
-            nc.vector.quantize_mx(g_words[:, cols].bitcast(E5M2), g_scales[:, cols], src)
+        def weave_g_on_vector(dst, src):
+            nc.vector.tensor_scalar(woven(dst), runs(src), -BETA, None, MULT)
 
-        def quant_w(s):
-            cols = slice(s * CH, (s + 1) * CH)
+        def quantise_g(lo, hi, src):
+            nc.vector.quantize_mx(g_words[:, lo:hi].bitcast(E5M2), g_scales[:, lo:hi], src)
+
+        def quantise_w(s):
+            cols = slice(s * CHUNK, (s + 1) * CHUNK)
             nc.vector.quantize_mx(w_words[:, cols].bitcast(E4M3), w_scales[:, cols], w_bf[s])
 
-        def product(m, lo, new, bank_tag, on_vector, res=None):
+        def product(m, lo, new, bank_tag, copy_out, queue=nc.sync, parts=1):
             rows = slice(m * P, (m + 1) * P)
             cols = slice(lo, lo + HALF)
             bank = psum.tile([P, HALF], F32, name=f"bank{m}_{lo}", tag=bank_tag)
@@ -114,50 +116,51 @@ def tile_attend_gvq_c_x_kernel(tc, zT, cb, wm, offs, out):
                 start=True,
                 stop=True,
             )
-            if res is None:
-                res = keep.tile([P, new], F32, name=f"res{m}_{lo}")[:]
-            if on_vector:
-                nc.vector.tensor_copy(res, bank[:, HALF - new : HALF])
-            else:
-                nc.scalar.copy(res, bank[:, HALF - new : HALF])
-            nc.sync.dma_start(out[rows, lo + HALF - new : lo + HALF], res)
-            return res
+            res = keep.tile([P, new], F32, name=f"res{m}_{lo}")
+            width = new // parts
+            for a in range(0, new, width):
+                in_bank = HALF - new + a
+                copy_out(res[:, a : a + width], bank[:, in_bank : in_bank + width])
+                queue.dma_start(out[rows, lo + in_bank : lo + in_bank + width], res[:, a : a + width])
 
-        look_up(0, 0, CH, z_head[:])
-        look_up(0, CH, HALF)
-        look_up(1, 0, HALF)
-        look_up(2, 0, HALF)
-        look_up(3, 0, CH)
-        look_up(3, CH, HALF)
-        weave_g(g_bf[0], diff_first[:, :, 0:CH], False)
-        weave_g(g_bf[1], diff_first[:, :, CH:HALF], False)
-        look_up(0, HALF, T)
-        quant_g(0, CH, g_bf[0])
-        quant_g(CH, CH, g_bf[1])
-        look_up(1, 2 * CH, 3 * CH)
+        for q in range(2):
+            look_up(0, q * CHUNK, (q + 1) * CHUNK, z_head[q][:])
+        for j in (1, 2):
+            look_up(j, 0, HALF, z_early[j][:])
+        for q in range(2):
+            look_up(3, q * CHUNK, (q + 1) * CHUNK, z_early[3][:, q * CHUNK : (q + 1) * CHUNK])
+        for q in range(2):
+            weave_g_on_scalar(
+                g_early[:, q * PACK * CHUNK : (q + 1) * PACK * CHUNK], diff_early[:, :, q * CHUNK : (q + 1) * CHUNK]
+            )
+
+        for j in (0, 1):
+            look_up(j, HALF, T, z_late[j])
+        quantise_g(0, HALF, g_early[:])
         for s in range(2):
-            nc.scalar.copy(woven(w_bf[s]), runs(w_raw[:, :, s * CH : (s + 1) * CH]))
-        quant_w(0)
-        look_up(1, 3 * CH, T)
-        look_up(2, 2 * CH, 3 * CH)
-        look_up(3, 2 * CH, 3 * CH)
-        quant_w(1)
-        look_up(2, 3 * CH, T)
-        look_up(3, 3 * CH, 3 * CH + 128)
-        look_up(3, 3 * CH + 128, T)
-        product(0, 0, HALF, "b0", False)
-        product(1, 0, HALF, "b1", False)
-        weave_g(g_bf[2], diff_late[:, :, 0:CH], False)
-        product(2, 0, HALF, "b2", False)
-        weave_g(g_last[0], diff_late[:, :, CH : CH + 128], False)
-        quant_g(2 * CH, CH, g_bf[2])
-        weave_g(g_last[1], diff_late[:, :, CH + 128 : HALF], True)
-        quant_g(3 * CH, 128, g_last[0])
-        quant_g(3 * CH + 128, 128, g_last[1])
-        product(3, 0, HALF, "b3", False)
-        product(0, CH, CH, "b4", True, g_last[1].bitcast(F32))
-        product(1, CH, CH, "b5", True, g_last[0].bitcast(F32))
-        product(2, HALF, HALF, "b6", True)
-        product(3, HALF, HALF, "b7", False)
-        product(0, HALF, CH, "b0", True)
-        product(1, HALF, CH, "b1", False)
+            nc.scalar.copy(woven(w_bf[s]), runs(w_raw[s][:]))
+        for s in range(2):
+            quantise_w(s)
+            for j in (2, 3):
+                look_up(j, HALF + s * CHUNK, HALF + (s + 1) * CHUNK, z_late[j][:, s * CHUNK : (s + 1) * CHUNK])
+
+        product(0, 0, HALF, "b0", nc.scalar.copy)
+        product(1, 0, HALF, "b1", nc.scalar.copy)
+        weave_g_on_scalar(g_late[:], diff_late[:, :, 0:CHUNK])
+        product(2, 0, HALF, "b2", nc.scalar.copy)
+        quantise_g(HALF, HALF + CHUNK, g_late[:])
+
+        pieces = [g_late[:, s * PACK * PIECE : (s + 1) * PACK * PIECE] for s in range(2)]
+        for s in range(2):
+            weave_g_on_vector(pieces[s], diff_late[:, :, CHUNK + s * PIECE : CHUNK + (s + 1) * PIECE])
+        for s in range(2):
+            quantise_g(HALF + CHUNK + s * PIECE, HALF + CHUNK + (s + 1) * PIECE, pieces[s])
+        product(3, 0, HALF, "b3", nc.scalar.copy)
+
+        product(0, CHUNK, CHUNK, "b4", nc.scalar.copy)
+        product(1, CHUNK, CHUNK, "b5", nc.scalar.copy)
+
+        product(2, HALF, HALF, "b6", nc.vector.tensor_copy, parts=2)
+        product(3, HALF, HALF, "b7", nc.scalar.copy)
+        product(0, HALF, CHUNK, "b0", nc.vector.tensor_copy)
+        product(1, HALF, CHUNK, "b1", nc.scalar.copy, queue=nc.scalar)

from contextlib import ExitStack

import concourse.mybir as mybir

T, C, D, DV = 1024, 512, 512, 512
BETA = 0.25
FLOPS = 2 * DV * D * T

F32 = mybir.dt.float32
BF16 = mybir.dt.bfloat16
U32 = mybir.dt.uint32
U16 = mybir.dt.uint16
U8 = mybir.dt.uint8
E4M3 = mybir.dt.float8_e4m3fn_x4
E5M2 = mybir.dt.float8_e5m2_x4
SUB = mybir.AluOpType.subtract
MULT = mybir.AluOpType.mult
COPY = mybir.ActivationFunctionType.Copy

P = 128
PACK = 4
BAND = 16
HALF = 512
CHUNK = 256
PIECE = 128
RUN = 4
STEP = HALF + CHUNK


def tile_attend_gvq_c_x_kernel(tc, zT, cb, wm, offs, out):
    nc = tc.nc
    with ExitStack() as ctx:
        lists = ctx.enter_context(tc.tile_pool(name="lists", bufs=1))
        keep = ctx.enter_context(tc.tile_pool(name="keep", bufs=1))
        psum = ctx.enter_context(tc.psum_pool(name="psum", bufs=1))

        codes = lists.tile([P, T // BAND], U16, name="codes")
        nc.sync.dma_start(codes[:], offs)

        cb_rows = cb.rearrange("(p j) c -> p j c", j=PACK)
        z_rows = zT.rearrange("(p j) t -> p j t", j=PACK)
        w_rows = wm.rearrange("(p j) d -> p j d", j=PACK)

        def planes(ap):
            return ap.rearrange("p (j c) -> p j c", j=PACK)

        shared = keep.tile([P, PACK * STEP], F32, name="shared", align_bytes=64)
        diff_late = planes(shared[:])[:, :, 0:HALF]
        diff_early = planes(keep.tile([P, PACK * HALF], F32, name="diff_early")[:])
        w_bf = [
            shared[:, lo : lo + PACK * CHUNK // 2].bitcast(BF16) for lo in (2 * STEP - CHUNK, 2 * STEP + CHUNK)
        ]

        book = [keep.tile([P, 2 * C], F32, name=f"book{j}") for j in range(PACK)]
        z_head = [keep.tile([P, CHUNK], F32, name=f"z_head{q}") for q in range(2)]
        z_early = {j: keep.tile([P, HALF], F32, name=f"z_early{j}") for j in range(1, PACK)}
        z_late = [keep.tile([P, HALF], F32, name=f"z_late{j}")[:] for j in (0, 1, 3)]
        z_late.insert(2, diff_late[:, 3, :])
        w_raw = [keep.tile([P, PACK, CHUNK], F32, name=f"w_raw{s}") for s in range(2)]

        for j in range(PACK):
            nc.gpsimd.memset(book[j][:, C : 2 * C], 0.0)
            nc.sync.dma_start(book[j][:, 0:C], cb_rows[:, j, :])
            if j == 0:
                for q in range(2):
                    nc.sync.dma_start(z_head[q][:], z_rows[:, 0, q * CHUNK : (q + 1) * CHUNK])
            else:
                nc.sync.dma_start(z_early[j][:], z_rows[:, j, 0:HALF])
        nc.sync.dma_start(z_late[0], z_rows[:, 0, HALF:T])
        nc.sync.dma_start(z_late[1], z_rows[:, 1, HALF:T])
        for s in range(2):
            nc.sync.dma_start(w_raw[s][:], w_rows[:, :, s * CHUNK : (s + 1) * CHUNK])
            nc.sync.dma_start(z_late[2 + s], z_rows[:, 2 + s, HALF:T])

        g_words = keep.tile([P, T], U32, name="g_words", align_bytes=64)
        g_scales = keep.tile([P, T], U8, name="g_scales", align_bytes=64)
        w_words = keep.tile([P, D], U32, name="w_words", align_bytes=64)
        w_scales = keep.tile([P, D], U8, name="w_scales", align_bytes=64)
        g_early = keep.tile([P, PACK * HALF], BF16, name="g_early", align_bytes=64)
        g_late = keep.tile([P, PACK * CHUNK], BF16, name="g_late", align_bytes=64)

        def look_up(j, lo, hi, z):
            half, first = divmod(lo, HALF)
            dst = (diff_early, diff_late)[half][:, j, first : first + hi - lo]
            nc.vector.tensor_tensor(dst, book[j][:].indirect(codes[:, lo // BAND : hi // BAND]), z, SUB)

        def woven(dst):
            return dst.rearrange("p (c i j) -> p c j i", i=RUN, j=PACK)

        def runs(src):
            return src.rearrange("p j (c i) -> p c j i", i=RUN)

        def weave_g_on_scalar(dst, src):
            nc.scalar.activation(woven(dst), runs(src), COPY, scale=-BETA)

        def weave_g_on_vector(dst, src):
            nc.vector.tensor_scalar(woven(dst), runs(src), -BETA, None, MULT)

        def quantise_g(lo, hi, src):
            nc.vector.quantize_mx(g_words[:, lo:hi].bitcast(E5M2), g_scales[:, lo:hi], src)

        def quantise_w(s):
            cols = slice(s * CHUNK, (s + 1) * CHUNK)
            nc.vector.quantize_mx(w_words[:, cols].bitcast(E4M3), w_scales[:, cols], w_bf[s])

        def product(m, lo, new, bank_tag, copy_out, queue=nc.sync, parts=1):
            rows = slice(m * P, (m + 1) * P)
            cols = slice(lo, lo + HALF)
            bank = psum.tile([P, HALF], F32, name=f"bank{m}_{lo}", tag=bank_tag)
            nc.tensor.matmul_mx(
                bank[:],
                lhsT=w_words[:, rows].bitcast(E4M3),
                lhsT_scale=w_scales[:, rows],
                rhs=g_words[:, cols].bitcast(E5M2),
                rhs_scale=g_scales[:, cols],
                start=True,
                stop=True,
            )
            res = keep.tile([P, new], F32, name=f"res{m}_{lo}")
            width = new // parts
            for a in range(0, new, width):
                in_bank = HALF - new + a
                copy_out(res[:, a : a + width], bank[:, in_bank : in_bank + width])
                queue.dma_start(out[rows, lo + in_bank : lo + in_bank + width], res[:, a : a + width])

        for q in range(2):
            look_up(0, q * CHUNK, (q + 1) * CHUNK, z_head[q][:])
        for j in (1, 2):
            look_up(j, 0, HALF, z_early[j][:])
        for q in range(2):
            look_up(3, q * CHUNK, (q + 1) * CHUNK, z_early[3][:, q * CHUNK : (q + 1) * CHUNK])
        for q in range(2):
            weave_g_on_scalar(
                g_early[:, q * PACK * CHUNK : (q + 1) * PACK * CHUNK], diff_early[:, :, q * CHUNK : (q + 1) * CHUNK]
            )

        for j in (0, 1):
            look_up(j, HALF, T, z_late[j])
        quantise_g(0, HALF, g_early[:])
        for s in range(2):
            nc.scalar.copy(woven(w_bf[s]), runs(w_raw[s][:]))
        for s in range(2):
            quantise_w(s)
            for j in (2, 3):
                look_up(j, HALF + s * CHUNK, HALF + (s + 1) * CHUNK, z_late[j][:, s * CHUNK : (s + 1) * CHUNK])

        product(0, 0, HALF, "b0", nc.scalar.copy)
        product(1, 0, HALF, "b1", nc.scalar.copy)
        weave_g_on_scalar(g_late[:], diff_late[:, :, 0:CHUNK])
        product(2, 0, HALF, "b2", nc.scalar.copy)
        quantise_g(HALF, HALF + CHUNK, g_late[:])

        pieces = [g_late[:, s * PACK * PIECE : (s + 1) * PACK * PIECE] for s in range(2)]
        for s in range(2):
            weave_g_on_vector(pieces[s], diff_late[:, :, CHUNK + s * PIECE : CHUNK + (s + 1) * PIECE])
        for s in range(2):
            quantise_g(HALF + CHUNK + s * PIECE, HALF + CHUNK + (s + 1) * PIECE, pieces[s])
        product(3, 0, HALF, "b3", nc.scalar.copy)

        product(0, CHUNK, CHUNK, "b4", nc.scalar.copy)
        product(1, CHUNK, CHUNK, "b5", nc.scalar.copy)

        product(2, HALF, HALF, "b6", nc.vector.tensor_copy, parts=2)
        product(3, HALF, HALF, "b7", nc.scalar.copy)
        product(0, HALF, CHUNK, "b0", nc.vector.tensor_copy)
        product(1, HALF, CHUNK, "b1", nc.scalar.copy, queue=nc.scalar)
